import numpy as np
import ml_dtypes


def mxq(x, axis, fmt="e4m3"):
    dtype, down = {"e4m3": (ml_dtypes.float8_e4m3fn, 7), "e5m2": (ml_dtypes.float8_e5m2, 14)}[fmt]
    v = np.moveaxis(np.asarray(x, np.float32).astype(ml_dtypes.bfloat16).astype(np.float64), axis, -1)
    blocks = v.reshape(v.shape[:-1] + (-1, 32))
    amax = np.abs(blocks).max(-1, keepdims=True)
    byte = np.maximum(np.where(amax > 0, np.frexp(amax)[1] - 1 + 127, 0) - down, 1)
    scale = np.exp2(byte - 127.0)
    codes = (blocks / scale).astype(np.float32).astype(dtype).astype(np.float64)
    return np.moveaxis((codes * scale).reshape(v.shape), -1, axis)


WIDE = False


def mx_kscale(k):
    if not WIDE:
        return np.ones(k)
    levels = np.array([10, -10, 5, -5, 0])
    if k % 512:
        return np.exp2(np.random.permutation(np.resize(levels, k // 32))).repeat(32)
    a = np.empty((k // 512, 16))
    for p in range(k // 512):
        a[p, :8] = np.random.permutation(np.resize(levels, 8))
        for g in range(8):
            far = levels[np.abs(levels - a[p, g]) >= 10]
            a[p, g + 8] = far[np.random.randint(len(far))]
    return np.exp2(a.ravel()).repeat(32)


def f64(x):
    return np.asarray(x).astype(np.float64)


def striped(idx):
    return np.tile(np.asarray(idx).reshape(-1, 16).T, (8, 1)).astype(np.uint16)


def unstriped(offs):
    return offs[:16].T.reshape(-1).astype(np.int64)


E2M1 = np.array([0.0, 0.5, 1.0, 1.5, 2.0, 3.0, 4.0, 6.0, -0.0, -0.5, -1.0, -1.5, -2.0, -3.0, -4.0, -6.0])


def pack_weight(w, fmt):
    k, n = w.shape
    w = f64(np.asarray(w, np.float32).astype(ml_dtypes.bfloat16)).reshape(k // 32, 32, n)
    amax = np.abs(w).max(1)
    if fmt == "e4m3":
        byte = np.frexp(amax)[1] - 1 + 127 - 7
    else:
        mant, ex = np.frexp(amax / 6.0)
        byte = np.where(mant > 0.5, ex, ex - 1) + 127
    byte = np.clip(np.where(amax > 0, byte, 1), 1, 254)
    scaled = (w * np.exp2(127.0 - byte)[:, None, :]).reshape(k, n).astype(np.float32)
    by_word = np.ascontiguousarray(scaled.reshape(k // 512, 128, 4, n).transpose(0, 1, 3, 2))
    if fmt == "e4m3":
        words = by_word.astype(ml_dtypes.float8_e4m3fn).view(np.uint8)
    else:
        c = by_word.astype(ml_dtypes.float4_e2m1fn).view(np.uint8) & 0xF
        words = (c[..., 0::2] | (c[..., 1::2] << 4)).reshape(k // 512, 128, 2 * n)
    return np.ascontiguousarray(words), np.ascontiguousarray(byte.astype(np.uint8).reshape(k // 512, 16, n))


def unpack_weight(words, scales, fmt):
    g, _, n = scales.shape
    words = np.ascontiguousarray(words).reshape(g, 128, n, -1)
    if fmt == "e4m3":
        vals = words.view(ml_dtypes.float8_e4m3fn).astype(np.float64)
    else:
        nib = np.empty((g, 128, n, 4), np.uint8)
        nib[..., 0::2] = words & 0xF
        nib[..., 1::2] = words >> 4
        vals = E2M1[nib]
    vals = vals * np.repeat(np.exp2(scales.astype(np.float64) - 127.0), 8, axis=1)[..., None]
    return vals.transpose(0, 1, 3, 2).reshape(g * 512, n)


R, D, T, I, U, V = 512, 512, 2048, 256, 1024, 1024


def setup_inputs():
    n = np.random.standard_normal
    idx = np.random.permutation(T)[:I]
    idx2 = np.random.permutation(U)[:I]
    idx3 = np.random.permutation(V)[:I]
    fr = mx_kscale(R)
    latp = pack_weight(n((R, T)) / fr[:, None], "e4m3")
    return {
        "up": (n((R, D)) * 0.8 / np.sqrt(R) * fr[:, None]).astype(np.float32),
        "lat_words": latp[0],
        "lat_scales": latp[1],
        "keys": (n((D, U))).astype(np.float32),
        "rate": (np.random.uniform(0.3, 1.0, (1, I))).astype(np.float32),
        "old": (n((D, V)) * 0.7).astype(np.float32),
        "fade": (np.random.uniform(0.5, 1.0, (1, V))).astype(np.float32),
        "offs": striped(idx),
        "offs2": striped(idx2),
        "offs3": striped(idx3),
    }


def reference(up, lat_words, lat_scales, keys, rate, old, fade, offs, offs2, offs3):
    idx = unstriped(offs)
    idx2 = unstriped(offs2)
    idx3 = unstriped(offs3)
    latu = unpack_weight(lat_words, lat_scales, "e4m3")
    upq = mxq(f64(up), 0, "e4m3")
    latidxg = latu[:, idx]
    z = upq.T @ latidxg
    rm = (f64(keys)[:, idx2] - z) * f64(rate)
    rf = np.zeros((D, V))
    rf[:, idx3] = rm
    y = f64(old) * f64(fade) + rf
    return y

@@ -1,0 +1,183 @@
+from contextlib import ExitStack
+
+import concourse.mybir as mybir
+from concourse.masks import make_identity
+
+R, D, T, I, U, V = 512, 512, 2048, 256, 1024, 1024
+FLOPS = 2 * R * D * I
+
+F32 = mybir.dt.float32
+BF16 = mybir.dt.bfloat16
+I32 = mybir.dt.int32
+U32 = mybir.dt.uint32
+U16 = mybir.dt.uint16
+U8 = mybir.dt.uint8
+FP8X4 = mybir.dt.float8_e4m3fn_x4
+ALU = mybir.AluOpType
+COPY = mybir.ActivationFunctionType.Copy
+
+P = 128
+PACK = 4
+TILES = D // P
+BANK = 512
+HALVES = V // BANK
+ORDER = ["s","l1","f","r","up","w","l2","k0","l3","k1","o0","k2","o1","k3","o2","o3"]
+GADD = [[0,0],[0,1],[1,0],[1,1]]
+VSCAT = []
+VG = [2,3]
+STEPS = [["r",0],["r",1],["m",0],["r",2],["m",1],["r",3],["m",2],["m",3],["a",0],["a",1],["a",2],["a",3]]
+SPLIT = [3]
+SSPLIT = [3]
+
+
+def tile_attend_remainderstore_kernel(tc, up, lat_words, lat_scales, keys, rate, old, fade, offs, offs2, offs3, out):
+    nc = tc.nc
+    with ExitStack() as ctx:
+        sb = ctx.enter_context(tc.tile_pool(name="sb", bufs=1))
+        ps = ctx.enter_context(tc.psum_pool(name="ps", bufs=1))
+
+        lat_list = sb.tile([P, I // 16], U16, name="lat_list")
+        key_list = sb.tile([P, I // 16], U16, name="key_list")
+        place_list = sb.tile([P, I // 16], U16, name="place_list")
+        up_raw = sb.tile([P, PACK, D], F32, name="up_raw")
+        words = sb.tile([P, T], U32, name="words", align_bytes=64)
+        scales = sb.tile([P, T], U8, name="scales", align_bytes=64)
+        fade_col = sb.tile([P, HALVES, PACK], F32, name="fade_col")
+        rate_col = sb.tile([P, 2], F32, name="rate_col")
+        key_t = [sb.tile([P, U], F32, name="key%d" % t) for t in range(TILES)]
+        old_t = [[sb.tile([P, BANK], F32, name="old%d_%d" % (t, h)) for h in range(HALVES)] if t in SPLIT else None for t in range(TILES)]
+        old_w = [None if t in SPLIT else sb.tile([P, V], F32, name="old%d" % t) for t in range(TILES)]
+        ident = sb.tile([P, P], F32, name="ident")
+
+        scale_rows = sb.tile([P, T // 4], I32, name="scale_rows", tag="grouped0", align_bytes=64)
+        nc.vector.memset(scales[:].bitcast(I32), 0)
+        for name in ORDER:
+            if name == "l1":
+                nc.sync.dma_start(lat_list[:], offs)
+            elif name == "s":
+                for r in range(4):
+                    nc.sync.dma_start(out=scale_rows[r:P:32, :], in_=lat_scales[0, r:16:4, :].bitcast(I32))
+            elif name == "f":
+                nc.sync.dma_start(out=fade_col[:], in_=fade.rearrange("o (h p j) -> p (o h) j", h=HALVES, j=PACK))
+            elif name == "r":
+                nc.sync.dma_start(out=rate_col[:], in_=rate.rearrange("o (p j) -> p (o j)", j=2))
+            elif name == "l2":
+                nc.sync.dma_start(key_list[:], offs2)
+            elif name == "l3":
+                nc.sync.dma_start(place_list[:], offs3)
+            elif name == "up":
+                nc.sync.dma_start(out=up_raw[:], in_=up.rearrange("(p j) d -> p j d", j=PACK))
+            elif name == "w":
+                nc.sync.dma_start(out=words[:].bitcast(I32), in_=lat_words[0].rearrange("p n t -> p (n t)").bitcast(I32))
+            elif name[0] == "k":
+                t = int(name[1])
+                nc.sync.dma_start(out=key_t[t][:], in_=keys[t * P : (t + 1) * P, :])
+            else:
+                t = int(name[1])
+                if t in SPLIT:
+                    for h in range(HALVES):
+                        nc.sync.dma_start(out=old_t[t][h][:], in_=old[t * P : (t + 1) * P, h * BANK : (h + 1) * BANK])
+                else:
+                    nc.sync.dma_start(out=old_w[t][:], in_=old[t * P : (t + 1) * P, :])
+
+        make_identity(nc, ident[:])
+
+        rate_ps = ps.tile([P, 2, P], F32, name="rate_ps")
+        for j in range(2):
+            nc.tensor.transpose(rate_ps[:, j, :], rate_col[:, j : j + 1].to_broadcast([P, P]), ident[:])
+        fade_ps = [ps.tile([P, PACK, P], F32, name="fade_ps%d" % h) for h in range(HALVES)]
+        for h in range(HALVES):
+            for j in range(PACK):
+                nc.tensor.transpose(fade_ps[h][:, j, :], fade_col[:, h, j : j + 1].to_broadcast([P, P]), ident[:])
+
+        for q in range(4):
+            nc.vector.tensor_copy(scales[32 * q : 32 * q + 4, :].bitcast(I32), scale_rows[32 * q : 32 * q + 4, :])
+        lat_s = sb.tile([P, I], U8, name="lat_s", align_bytes=64)
+        nc.vector.tensor_copy(lat_s[:], scales[:].indirect(lat_list[:]))
+
+        W = D // 2
+        grouped = [sb.tile([P, W, PACK], BF16, name="grouped%d" % c, tag="grouped%d" % c, align_bytes=64) for c in range(2)]
+        up_q = [sb.tile([P, W], U32, name="up_q%d" % c, tag="up_q%d" % c, align_bytes=64) for c in range(2)]
+        up_s = [sb.tile([P, W], U8, name="up_s%d" % c, align_bytes=64) for c in range(2)]
+        for c in range(2):
+            (nc.vector.tensor_copy if c == 0 else nc.scalar.copy)(
+                out=grouped[c][:].rearrange("p (c i) t -> p c t i", i=4),
+                in_=up_raw[:, :, c * W : (c + 1) * W].rearrange("p t (c i) -> p c t i", i=4),
+            )
+        for c in range(2):
+            nc.vector.quantize_mx(out=up_q[c][:].bitcast(FP8X4), scales=up_s[c][:], in_=grouped[c][:].rearrange("p w t -> p (w t)"))
+
+        lat_q = sb.tile([P, I], U32, name="lat_q", tag="grouped1", align_bytes=64)
+        nc.vector.tensor_copy(lat_q[:], words[:].indirect(lat_list[:]))
+
+        z01 = [ps.tile([P, I], F32, name="z%d" % t) for t in range(2)]
+        z23 = ps.tile([P, 2, I], F32, name="z23")
+        z = [z01[0][:], z01[1][:], z23[:, 0, :], z23[:, 1, :]]
+        for t in range(TILES):
+            cols = slice((t % 2) * P, (t % 2 + 1) * P)
+            nc.tensor.matmul_mx(
+                out=z[t],
+                lhsT=up_q[t // 2][:, cols].bitcast(FP8X4),
+                lhsT_scale=up_s[t // 2][:, cols],
+                rhs=lat_q[:].bitcast(FP8X4),
+                rhs_scale=lat_s[:],
+                start=True,
+                stop=True,
+            )
+        rf = [sb.tile([P, V], F32, name="rf%d" % t) for t in range(2)]
+        rf.extend([sb.tile([P, V], F32, name="rf%d" % (2 + c), tag="up_q%d" % c, align_bytes=64) for c in range(2)])
+        for t in range(TILES):
+            (nc.vector if t < 2 else nc.gpsimd).memset(rf[t][:], 0.0)
+        z_sb = sb.tile([P, 2, I], F32, name="z_sb")
+        diff = [sb.tile([P, I], F32, name="diff%d" % t, tag="work%d" % t) for t in range(TILES)]
+        picked = [sb.tile([P, I], F32, name="picked%d" % t) for t in range(TILES)]
+        rm = [sb.tile([P, I], F32, name="rm%d" % t) for t in range(TILES)]
+        faded = {}
+        res = [sb.tile([P, V], F32, name="res%d" % t) for t in range(TILES)]
+
+        def remainder(t):
+            if t in VG:
+                nc.vector.tensor_tensor(diff[t][:], key_t[t][:].indirect(key_list[:]), z_sb[:, t - 2, :], ALU.subtract)
+            else:
+                nc.vector.tensor_tensor(diff[t][:], picked[t][:], z[t], ALU.subtract)
+            nc.vector.tensor_tensor(
+                rm[t][:].rearrange("q (p j) -> q p j", j=2),
+                diff[t][:].rearrange("q (p j) -> q p j", j=2),
+                rate_ps[:].rearrange("q j p -> q p j"),
+                ALU.mult,
+            )
+            nc.scalar.activation(rf[t][:].indirect(place_list[:]), rm[t][:], COPY)
+
+        def fade_old(t):
+            faded[t] = sb.tile([P, V], F32, name="faded%d" % t, tag="work%d" % t)
+            for h in range(HALVES):
+                src = old_t[t][h][:] if t in SPLIT else old_w[t][:, h * BANK : (h + 1) * BANK]
+                nc.vector.tensor_tensor(
+                    faded[t][:, h * BANK : (h + 1) * BANK].rearrange("q (p j) -> q p j", j=PACK),
+                    src.rearrange("q (p j) -> q p j", j=PACK),
+                    fade_ps[h][:].rearrange("q j p -> q p j"),
+                    ALU.mult,
+                )
+
+        def finish(t):
+            for h in range(HALVES):
+                cols = slice(h * BANK, (h + 1) * BANK)
+                eng = nc.gpsimd if [t, h] in GADD else nc.vector
+                eng.tensor_tensor(res[t][:, cols], faded[t][:, cols], rf[t][:, cols], ALU.add)
+                if t in SSPLIT:
+                    nc.sync.dma_start(out=out[t * P : (t + 1) * P, cols], in_=res[t][:, cols])
+            if t not in SSPLIT:
+                nc.sync.dma_start(out=out[t * P : (t + 1) * P, :], in_=res[t][:])
+
+        for t in range(TILES):
+            if t not in VG:
+                nc.scalar.activation(picked[t][:], key_t[t][:].indirect(key_list[:]), COPY)
+            if t == 0 and len(VG) > 0:
+                nc.scalar.activation(z_sb[:], z23[:], COPY)
+        for kind, t in STEPS:
+            if kind == "r":
+                remainder(t)
+            elif kind == "m":
+                fade_old(t)
+            else:
+                finish(t)

@@ -44,7 +44,7 @@ def tile_attend_remainderstore_kernel(tc, up, lat_words, lat_scales, keys, rate,
         scales = sb.tile([P, T], U8, name="scales", align_bytes=64)
         fade_col = sb.tile([P, HALVES, PACK], F32, name="fade_col")
         rate_col = sb.tile([P, 2], F32, name="rate_col")
-        key_t = [sb.tile([P, U], F32, name="key%d" % t) for t in range(TILES)]
+        key_t = [sb.tile([P, U], F32, name="key%d" % t, tag="key%d" % t) for t in range(TILES)]
         old_t = [[sb.tile([P, BANK], F32, name="old%d_%d" % (t, h)) for h in range(HALVES)] if t in SPLIT else None for t in range(TILES)]
         old_w = [None if t in SPLIT else sb.tile([P, V], F32, name="old%d" % t) for t in range(TILES)]
         ident = sb.tile([P, P], F32, name="ident")
@@ -128,8 +128,7 @@ def tile_attend_remainderstore_kernel(tc, up, lat_words, lat_scales, keys, rate,
         rf.extend([sb.tile([P, V], F32, name="rf%d" % (2 + c), tag="up_q%d" % c, align_bytes=64) for c in range(2)])
         for t in range(TILES):
             (nc.vector if t < 2 else nc.gpsimd).memset(rf[t][:], 0.0)
-        z_sb = sb.tile([P, 2, I], F32, name="z_sb")
-        diff = [sb.tile([P, I], F32, name="diff%d" % t, tag="work%d" % t) for t in range(TILES)]
+        diff = [sb.tile([P, I], F32, name="diff%d" % t) for t in range(TILES)]
         picked = [sb.tile([P, I], F32, name="picked%d" % t) for t in range(TILES)]
         rm = [sb.tile([P, I], F32, name="rm%d" % t) for t in range(TILES)]
         faded = {}
@@ -149,7 +148,7 @@ def tile_attend_remainderstore_kernel(tc, up, lat_words, lat_scales, keys, rate,
             nc.scalar.activation(rf[t][:].indirect(place_list[:]), rm[t][:], COPY)
 
         def fade_old(t):
-            faded[t] = sb.tile([P, V], F32, name="faded%d" % t, tag="work%d" % t)
+            faded[t] = sb.tile([P, V], F32, name="faded%d" % t)
             for h in range(HALVES):
                 src = old_t[t][h][:] if t in SPLIT else old_w[t][:, h * BANK : (h + 1) * BANK]
                 nc.vector.tensor_tensor(
@@ -172,8 +171,8 @@ def tile_attend_remainderstore_kernel(tc, up, lat_words, lat_scales, keys, rate,
         for t in range(TILES):
             if t not in VG:
                 nc.scalar.activation(picked[t][:], key_t[t][:].indirect(key_list[:]), COPY)
-            if t == 0 and len(VG) > 0:
-                nc.scalar.activation(z_sb[:], z23[:], COPY)
+        z_sb = sb.tile([P, 2, I], F32, name="z_sb", tag="key0")
+        nc.scalar.activation(z_sb[:], z23[:], COPY)
         for kind, t in STEPS:
             if kind == "r":
                 remainder(t)

@@ -21,11 +21,11 @@ PACK = 4
 TILES = D // P
 BANK = 512
 HALVES = V // BANK
-ORDER = ["s","l1","f","r","up","w","l2","k0","l3","k1","o0","k2","o1","k3","o2","o3"]
+ORDER = ["s","l1","f","r","up","w","o0","l2","k0","l3","k1","o1","k2","k3","o2","o3"]
 GADD = [[0,0],[0,1],[1,0],[1,1]]
 VSCAT = []
 VG = [2,3]
-STEPS = [["r",0],["r",1],["m",0],["r",2],["m",1],["r",3],["m",2],["m",3],["a",0],["a",1],["a",2],["a",3]]
+STEPS = [["m",0],["r",0],["r",1],["m",1],["r",2],["r",3],["m",2],["m",3],["a",0],["a",1],["a",2],["a",3]]
 SPLIT = [3]
 SSPLIT = [3]
 

@@ -3,8 +3,8 @@ from contextlib import ExitStack
 import concourse.mybir as mybir
 from concourse.masks import make_identity
 
-R, D, T, I, U, V = 512, 512, 2048, 256, 1024, 1024
-FLOPS = 2 * R * D * I
+R, D, T, SLOTS, U, V = 512, 512, 2048, 256, 1024, 1024
+FLOPS = 2 * R * D * SLOTS
 
 F32 = mybir.dt.float32
 BF16 = mybir.dt.bfloat16
@@ -18,16 +18,14 @@ COPY = mybir.ActivationFunctionType.Copy
 
 P = 128
 PACK = 4
+QUADRANTS = P // 32
 TILES = D // P
 BANK = 512
 HALVES = V // BANK
-ORDER = ["s","l1","f","r","up","w","o0","l2","k0","l3","k1","o1","k2","k3","o2","o3"]
-GADD = [[0,0],[0,1],[1,0],[1,1]]
-VSCAT = []
-VG = [2,3]
-STEPS = [["m",0],["r",0],["r",1],["m",1],["r",2],["r",3],["m",2],["m",3],["a",0],["a",1],["a",2],["a",3]]
-SPLIT = [3]
-SSPLIT = [3]
+FADE_RUN = BANK // P
+RATE_RUN = SLOTS // P
+UP_COLS = D // 2
+EARLY = 2
 
 
 def tile_attend_remainderstore_kernel(tc, up, lat_words, lat_scales, keys, rate, old, fade, offs, offs2, offs3, out):
@@ -36,87 +34,81 @@ def tile_attend_remainderstore_kernel(tc, up, lat_words, lat_scales, keys, rate,
         sb = ctx.enter_context(tc.tile_pool(name="sb", bufs=1))
         ps = ctx.enter_context(tc.psum_pool(name="ps", bufs=1))
 
-        lat_list = sb.tile([P, I // 16], U16, name="lat_list")
-        key_list = sb.tile([P, I // 16], U16, name="key_list")
-        place_list = sb.tile([P, I // 16], U16, name="place_list")
+        def rows(t):
+            return slice(t * P, (t + 1) * P)
+
+        def half(h):
+            return slice(h * BANK, (h + 1) * BANK)
+
+        lat_list = sb.tile([P, SLOTS // 16], U16, name="lat_list")
+        key_list = sb.tile([P, SLOTS // 16], U16, name="key_list")
+        place_list = sb.tile([P, SLOTS // 16], U16, name="place_list")
         up_raw = sb.tile([P, PACK, D], F32, name="up_raw")
         words = sb.tile([P, T], U32, name="words", align_bytes=64)
         scales = sb.tile([P, T], U8, name="scales", align_bytes=64)
-        fade_col = sb.tile([P, HALVES, PACK], F32, name="fade_col")
-        rate_col = sb.tile([P, 2], F32, name="rate_col")
-        key_t = [sb.tile([P, U], F32, name="key%d" % t, tag="key%d" % t) for t in range(TILES)]
-        old_t = [[sb.tile([P, BANK], F32, name="old%d_%d" % (t, h)) for h in range(HALVES)] if t in SPLIT else None for t in range(TILES)]
-        old_w = [None if t in SPLIT else sb.tile([P, V], F32, name="old%d" % t) for t in range(TILES)]
+        scale_rows = sb.tile([P, T // 4], I32, name="scale_rows", tag="grouped0", align_bytes=64)
+        fade_col = sb.tile([P, HALVES, FADE_RUN], F32, name="fade_col")
+        rate_col = sb.tile([P, RATE_RUN], F32, name="rate_col")
+        key = [sb.tile([P, U], F32, name="key%d" % t, tag="key%d" % t) for t in range(TILES)]
+        last = TILES - 1
+        old_whole = [sb.tile([P, V], F32, name="old%d" % t, tag="old%d" % t) for t in range(last)]
+        old_last = [sb.tile([P, BANK], F32, name="old_last%d" % h, tag="old_last%d" % h) for h in range(HALVES)]
         ident = sb.tile([P, P], F32, name="ident")
 
-        scale_rows = sb.tile([P, T // 4], I32, name="scale_rows", tag="grouped0", align_bytes=64)
-        nc.vector.memset(scales[:].bitcast(I32), 0)
-        for name in ORDER:
-            if name == "l1":
-                nc.sync.dma_start(lat_list[:], offs)
-            elif name == "s":
-                for r in range(4):
-                    nc.sync.dma_start(out=scale_rows[r:P:32, :], in_=lat_scales[0, r:16:4, :].bitcast(I32))
-            elif name == "f":
-                nc.sync.dma_start(out=fade_col[:], in_=fade.rearrange("o (h p j) -> p (o h) j", h=HALVES, j=PACK))
-            elif name == "r":
-                nc.sync.dma_start(out=rate_col[:], in_=rate.rearrange("o (p j) -> p (o j)", j=2))
-            elif name == "l2":
-                nc.sync.dma_start(key_list[:], offs2)
-            elif name == "l3":
-                nc.sync.dma_start(place_list[:], offs3)
-            elif name == "up":
-                nc.sync.dma_start(out=up_raw[:], in_=up.rearrange("(p j) d -> p j d", j=PACK))
-            elif name == "w":
-                nc.sync.dma_start(out=words[:].bitcast(I32), in_=lat_words[0].rearrange("p n t -> p (n t)").bitcast(I32))
-            elif name[0] == "k":
-                t = int(name[1])
-                nc.sync.dma_start(out=key_t[t][:], in_=keys[t * P : (t + 1) * P, :])
-            else:
-                t = int(name[1])
-                if t in SPLIT:
-                    for h in range(HALVES):
-                        nc.sync.dma_start(out=old_t[t][h][:], in_=old[t * P : (t + 1) * P, h * BANK : (h + 1) * BANK])
-                else:
-                    nc.sync.dma_start(out=old_w[t][:], in_=old[t * P : (t + 1) * P, :])
-
-        make_identity(nc, ident[:])
-
-        rate_ps = ps.tile([P, 2, P], F32, name="rate_ps")
-        for j in range(2):
-            nc.tensor.transpose(rate_ps[:, j, :], rate_col[:, j : j + 1].to_broadcast([P, P]), ident[:])
-        fade_ps = [ps.tile([P, PACK, P], F32, name="fade_ps%d" % h) for h in range(HALVES)]
+        for j in range(4):
+            nc.sync.dma_start(out=scale_rows[j:P:32, :], in_=lat_scales[0, j:16:4, :].bitcast(I32))
+        nc.sync.dma_start(lat_list[:], offs)
+        nc.sync.dma_start(out=fade_col[:], in_=fade.rearrange("o (h p j) -> p (o h) j", h=HALVES, j=FADE_RUN))
+        nc.sync.dma_start(out=rate_col[:], in_=rate.rearrange("o (p j) -> p (o j)", j=RATE_RUN))
+        nc.sync.dma_start(out=up_raw[:], in_=up.rearrange("(p j) d -> p j d", j=PACK))
+        nc.sync.dma_start(out=words[:].bitcast(I32), in_=lat_words[0].rearrange("p n j -> p (n j)").bitcast(I32))
+        nc.sync.dma_start(out=old_whole[0][:], in_=old[rows(0), :])
+        nc.sync.dma_start(key_list[:], offs2)
+        nc.sync.dma_start(out=key[0][:], in_=keys[rows(0), :])
+        nc.sync.dma_start(place_list[:], offs3)
+        nc.sync.dma_start(out=key[1][:], in_=keys[rows(1), :])
+        nc.sync.dma_start(out=old_whole[1][:], in_=old[rows(1), :])
+        for t in range(EARLY, TILES):
+            nc.sync.dma_start(out=key[t][:], in_=keys[rows(t), :])
+        nc.sync.dma_start(out=old_whole[2][:], in_=old[rows(2), :])
         for h in range(HALVES):
-            for j in range(PACK):
+            nc.sync.dma_start(out=old_last[h][:], in_=old[rows(last), half(h)])
+
+        nc.vector.memset(scales[:].bitcast(I32), 0)
+        make_identity(nc, ident[:])
+        rate_ps = ps.tile([P, RATE_RUN, P], F32, name="rate_ps")
+        for j in range(RATE_RUN):
+            nc.tensor.transpose(rate_ps[:, j, :], rate_col[:, j : j + 1].to_broadcast([P, P]), ident[:])
+        fade_ps = [ps.tile([P, FADE_RUN, P], F32, name="fade_ps%d" % h) for h in range(HALVES)]
+        for h in range(HALVES):
+            for j in range(FADE_RUN):
                 nc.tensor.transpose(fade_ps[h][:, j, :], fade_col[:, h, j : j + 1].to_broadcast([P, P]), ident[:])
 
-        for q in range(4):
+        for q in range(QUADRANTS):
             nc.vector.tensor_copy(scales[32 * q : 32 * q + 4, :].bitcast(I32), scale_rows[32 * q : 32 * q + 4, :])
-        lat_s = sb.tile([P, I], U8, name="lat_s", align_bytes=64)
+        lat_s = sb.tile([P, SLOTS], U8, name="lat_s", align_bytes=64)
         nc.vector.tensor_copy(lat_s[:], scales[:].indirect(lat_list[:]))
 
-        W = D // 2
-        grouped = [sb.tile([P, W, PACK], BF16, name="grouped%d" % c, tag="grouped%d" % c, align_bytes=64) for c in range(2)]
-        up_q = [sb.tile([P, W], U32, name="up_q%d" % c, tag="up_q%d" % c, align_bytes=64) for c in range(2)]
-        up_s = [sb.tile([P, W], U8, name="up_s%d" % c, align_bytes=64) for c in range(2)]
-        for c in range(2):
-            (nc.vector.tensor_copy if c == 0 else nc.scalar.copy)(
-                out=grouped[c][:].rearrange("p (c i) t -> p c t i", i=4),
-                in_=up_raw[:, :, c * W : (c + 1) * W].rearrange("p t (c i) -> p c t i", i=4),
+        grouped = [sb.tile([P, UP_COLS, PACK], BF16, name="grouped%d" % c, tag="grouped%d" % c, align_bytes=64) for c in range(2)]
+        up_q = [sb.tile([P, UP_COLS], U32, name="up_q%d" % c, tag="up_q%d" % c, align_bytes=64) for c in range(2)]
+        up_s = [sb.tile([P, UP_COLS], U8, name="up_s%d" % c, align_bytes=64) for c in range(2)]
+        for c, copy in enumerate((nc.vector.tensor_copy, nc.scalar.copy)):
+            copy(
+                out=grouped[c][:].rearrange("p (w i) j -> p w j i", i=4),
+                in_=up_raw[:, :, c * UP_COLS : (c + 1) * UP_COLS].rearrange("p j (w i) -> p w j i", i=4),
             )
         for c in range(2):
-            nc.vector.quantize_mx(out=up_q[c][:].bitcast(FP8X4), scales=up_s[c][:], in_=grouped[c][:].rearrange("p w t -> p (w t)"))
+            nc.vector.quantize_mx(out=up_q[c][:].bitcast(FP8X4), scales=up_s[c][:], in_=grouped[c][:].rearrange("p w j -> p (w j)"))
 
-        lat_q = sb.tile([P, I], U32, name="lat_q", tag="grouped1", align_bytes=64)
+        lat_q = sb.tile([P, SLOTS], U32, name="lat_q", tag="grouped1", align_bytes=64)
         nc.vector.tensor_copy(lat_q[:], words[:].indirect(lat_list[:]))
 
-        z01 = [ps.tile([P, I], F32, name="z%d" % t) for t in range(2)]
-        z23 = ps.tile([P, 2, I], F32, name="z23")
-        z = [z01[0][:], z01[1][:], z23[:, 0, :], z23[:, 1, :]]
+        z_early = [ps.tile([P, SLOTS], F32, name="z%d" % t) for t in range(EARLY)]
+        z_late = ps.tile([P, TILES - EARLY, SLOTS], F32, name="z_late")
         for t in range(TILES):
-            cols = slice((t % 2) * P, (t % 2 + 1) * P)
+            cols = rows(t % 2)
             nc.tensor.matmul_mx(
-                out=z[t],
+                out=z_early[t][:] if t < EARLY else z_late[:, t - EARLY, :],
                 lhsT=up_q[t // 2][:, cols].bitcast(FP8X4),
                 lhsT_scale=up_s[t // 2][:, cols],
                 rhs=lat_q[:].bitcast(FP8X4),
@@ -124,59 +116,57 @@ def tile_attend_remainderstore_kernel(tc, up, lat_words, lat_scales, keys, rate,
                 start=True,
                 stop=True,
             )
-        rf = [sb.tile([P, V], F32, name="rf%d" % t) for t in range(2)]
-        rf.extend([sb.tile([P, V], F32, name="rf%d" % (2 + c), tag="up_q%d" % c, align_bytes=64) for c in range(2)])
-        for t in range(TILES):
-            (nc.vector if t < 2 else nc.gpsimd).memset(rf[t][:], 0.0)
-        diff = [sb.tile([P, I], F32, name="diff%d" % t) for t in range(TILES)]
-        picked = [sb.tile([P, I], F32, name="picked%d" % t) for t in range(TILES)]
-        rm = [sb.tile([P, I], F32, name="rm%d" % t) for t in range(TILES)]
-        faded = {}
-        res = [sb.tile([P, V], F32, name="res%d" % t) for t in range(TILES)]
 
-        def remainder(t):
-            if t in VG:
-                nc.vector.tensor_tensor(diff[t][:], key_t[t][:].indirect(key_list[:]), z_sb[:, t - 2, :], ALU.subtract)
+        rf = [sb.tile([P, V], F32, name="rf%d" % t) for t in range(EARLY)]
+        rf.extend([sb.tile([P, V], F32, name="rf%d" % (EARLY + c), tag="up_q%d" % c, align_bytes=64) for c in range(2)])
+        for t in range(TILES):
+            (nc.vector if t < EARLY else nc.gpsimd).memset(rf[t][:], 0.0)
+
+        picked = [sb.tile([P, SLOTS], F32, name="picked%d" % t) for t in range(EARLY)]
+        for t in range(EARLY):
+            nc.scalar.activation(picked[t][:], key[t][:].indirect(key_list[:]), COPY)
+        z_sb = sb.tile([P, TILES - EARLY, SLOTS], F32, name="z_sb", tag="key0")
+        nc.scalar.activation(z_sb[:], z_late[:], COPY)
+
+        def remainder(t, diff_tag):
+            diff = sb.tile([P, SLOTS], F32, name="diff%d" % t, tag=diff_tag)
+            if t < EARLY:
+                nc.vector.tensor_tensor(diff[:], picked[t][:], z_early[t][:], ALU.subtract)
             else:
-                nc.vector.tensor_tensor(diff[t][:], picked[t][:], z[t], ALU.subtract)
+                nc.vector.tensor_tensor(diff[:], key[t][:].indirect(key_list[:]), z_sb[:, t - EARLY, :], ALU.subtract)
+            rm = sb.tile([P, SLOTS], F32, name="rm%d" % t)
             nc.vector.tensor_tensor(
-                rm[t][:].rearrange("q (p j) -> q p j", j=2),
-                diff[t][:].rearrange("q (p j) -> q p j", j=2),
+                rm[:].rearrange("q (p j) -> q p j", j=RATE_RUN),
+                diff[:].rearrange("q (p j) -> q p j", j=RATE_RUN),
                 rate_ps[:].rearrange("q j p -> q p j"),
                 ALU.mult,
             )
-            nc.scalar.activation(rf[t][:].indirect(place_list[:]), rm[t][:], COPY)
+            nc.scalar.activation(rf[t][:].indirect(place_list[:]), rm[:], COPY)
 
-        def fade_old(t):
-            faded[t] = sb.tile([P, V], F32, name="faded%d" % t)
+        def fading(t, faded_tag):
+            faded = sb.tile([P, V], F32, name="faded%d" % t, tag=faded_tag)
             for h in range(HALVES):
-                src = old_t[t][h][:] if t in SPLIT else old_w[t][:, h * BANK : (h + 1) * BANK]
+                src = old_last[h][:] if t == last else old_whole[t][:, half(h)]
                 nc.vector.tensor_tensor(
-                    faded[t][:, h * BANK : (h + 1) * BANK].rearrange("q (p j) -> q p j", j=PACK),
-                    src.rearrange("q (p j) -> q p j", j=PACK),
+                    faded[:, half(h)].rearrange("q (p j) -> q p j", j=FADE_RUN),
+                    src.rearrange("q (p j) -> q p j", j=FADE_RUN),
                     fade_ps[h][:].rearrange("q j p -> q p j"),
                     ALU.mult,
                 )
+            return faded
 
-        def finish(t):
-            for h in range(HALVES):
-                cols = slice(h * BANK, (h + 1) * BANK)
-                eng = nc.gpsimd if [t, h] in GADD else nc.vector
-                eng.tensor_tensor(res[t][:, cols], faded[t][:, cols], rf[t][:, cols], ALU.add)
-                if t in SSPLIT:
-                    nc.sync.dma_start(out=out[t * P : (t + 1) * P, cols], in_=res[t][:, cols])
-            if t not in SSPLIT:
-                nc.sync.dma_start(out=out[t * P : (t + 1) * P, :], in_=res[t][:])
+        faded = [fading(0, "faded0")]
+        remainder(0, "diff0")
+        remainder(1, "diff1")
+        faded.append(fading(1, "diff0"))
+        remainder(2, "diff1")
+        remainder(3, "old1")
+        faded.append(fading(2, "key3"))
+        faded.append(fading(3, "old1"))
 
         for t in range(TILES):
-            if t not in VG:
-                nc.scalar.activation(picked[t][:], key_t[t][:].indirect(key_list[:]), COPY)
-        z_sb = sb.tile([P, 2, I], F32, name="z_sb", tag="key0")
-        nc.scalar.activation(z_sb[:], z23[:], COPY)
-        for kind, t in STEPS:
-            if kind == "r":
-                remainder(t)
-            elif kind == "m":
-                fade_old(t)
-            else:
-                finish(t)
+            for h in range(HALVES):
+                res = sb.tile([P, BANK], F32, name="res%d_%d" % (t, h), tag="old_last%d" % h if t == EARLY else "res%d_%d" % (t, h))
+                engine = nc.gpsimd if t < EARLY else nc.vector
+                engine.tensor_tensor(res[:], faded[t][:, half(h)], rf[t][:, half(h)], ALU.add)
+                nc.sync.dma_start(out=out[rows(t), half(h)], in_=res[:])

@@ -51,7 +51,7 @@ def tile_attend_remainderstore_kernel(tc, up, lat_words, lat_scales, keys, rate,
         rate_col = sb.tile([P, RATE_RUN], F32, name="rate_col")
         key = [sb.tile([P, U], F32, name="key%d" % t, tag="key%d" % t) for t in range(TILES)]
         last = TILES - 1
-        old_whole = [sb.tile([P, V], F32, name="old%d" % t, tag="old%d" % t) for t in range(last)]
+        old_whole = [sb.tile([P, V], F32, name="old%d" % t) for t in range(last)]
         old_last = [sb.tile([P, BANK], F32, name="old_last%d" % h, tag="old_last%d" % h) for h in range(HALVES)]
         ident = sb.tile([P, P], F32, name="ident")
 
@@ -66,11 +66,10 @@ def tile_attend_remainderstore_kernel(tc, up, lat_words, lat_scales, keys, rate,
         nc.sync.dma_start(key_list[:], offs2)
         nc.sync.dma_start(out=key[0][:], in_=keys[rows(0), :])
         nc.sync.dma_start(place_list[:], offs3)
-        nc.sync.dma_start(out=key[1][:], in_=keys[rows(1), :])
-        nc.sync.dma_start(out=old_whole[1][:], in_=old[rows(1), :])
-        for t in range(EARLY, TILES):
+        for t in range(1, TILES):
             nc.sync.dma_start(out=key[t][:], in_=keys[rows(t), :])
-        nc.sync.dma_start(out=old_whole[2][:], in_=old[rows(2), :])
+        for t in range(1, last):
+            nc.sync.dma_start(out=old_whole[t][:], in_=old[rows(t), :])
         for h in range(HALVES):
             nc.sync.dma_start(out=old_last[h][:], in_=old[rows(last), half(h)])
 
@@ -128,8 +127,8 @@ def tile_attend_remainderstore_kernel(tc, up, lat_words, lat_scales, keys, rate,
         z_sb = sb.tile([P, TILES - EARLY, SLOTS], F32, name="z_sb", tag="key0")
         nc.scalar.activation(z_sb[:], z_late[:], COPY)
 
-        def remainder(t, diff_tag):
-            diff = sb.tile([P, SLOTS], F32, name="diff%d" % t, tag=diff_tag)
+        def remainder(t):
+            diff = sb.tile([P, SLOTS], F32, name="diff%d" % t)
             if t < EARLY:
                 nc.vector.tensor_tensor(diff[:], picked[t][:], z_early[t][:], ALU.subtract)
             else:
@@ -143,8 +142,8 @@ def tile_attend_remainderstore_kernel(tc, up, lat_words, lat_scales, keys, rate,
             )
             nc.scalar.activation(rf[t][:].indirect(place_list[:]), rm[:], COPY)
 
-        def fading(t, faded_tag):
-            faded = sb.tile([P, V], F32, name="faded%d" % t, tag=faded_tag)
+        def fading(t):
+            faded = sb.tile([P, V], F32, name="faded%d" % t)
             for h in range(HALVES):
                 src = old_last[h][:] if t == last else old_whole[t][:, half(h)]
                 nc.vector.tensor_tensor(
@@ -155,14 +154,10 @@ def tile_attend_remainderstore_kernel(tc, up, lat_words, lat_scales, keys, rate,
                 )
             return faded
 
-        faded = [fading(0, "faded0")]
-        remainder(0, "diff0")
-        remainder(1, "diff1")
-        faded.append(fading(1, "diff0"))
-        remainder(2, "diff1")
-        remainder(3, "old1")
-        faded.append(fading(2, "key3"))
-        faded.append(fading(3, "old1"))
+        faded = [fading(0)]
+        for t in range(TILES):
+            remainder(t)
+        faded.extend([fading(t) for t in range(1, TILES)])
 
         for t in range(TILES):
             for h in range(HALVES):

from contextlib import ExitStack

import concourse.mybir as mybir
from concourse.masks import make_identity

R, D, T, SLOTS, U, V = 512, 512, 2048, 256, 1024, 1024
FLOPS = 2 * R * D * SLOTS

F32 = mybir.dt.float32
BF16 = mybir.dt.bfloat16
I32 = mybir.dt.int32
U32 = mybir.dt.uint32
U16 = mybir.dt.uint16
U8 = mybir.dt.uint8
FP8X4 = mybir.dt.float8_e4m3fn_x4
ALU = mybir.AluOpType
COPY = mybir.ActivationFunctionType.Copy

P = 128
PACK = 4
QUADRANTS = P // 32
TILES = D // P
BANK = 512
HALVES = V // BANK
FADE_RUN = BANK // P
RATE_RUN = SLOTS // P
UP_COLS = D // 2
EARLY = 2


def tile_attend_remainderstore_kernel(tc, up, lat_words, lat_scales, keys, rate, old, fade, offs, offs2, offs3, out):
    nc = tc.nc
    with ExitStack() as ctx:
        sb = ctx.enter_context(tc.tile_pool(name="sb", bufs=1))
        ps = ctx.enter_context(tc.psum_pool(name="ps", bufs=1))

        def rows(t):
            return slice(t * P, (t + 1) * P)

        def half(h):
            return slice(h * BANK, (h + 1) * BANK)

        lat_list = sb.tile([P, SLOTS // 16], U16, name="lat_list")
        key_list = sb.tile([P, SLOTS // 16], U16, name="key_list")
        place_list = sb.tile([P, SLOTS // 16], U16, name="place_list")
        up_raw = sb.tile([P, PACK, D], F32, name="up_raw")
        words = sb.tile([P, T], U32, name="words", align_bytes=64)
        scales = sb.tile([P, T], U8, name="scales", align_bytes=64)
        scale_rows = sb.tile([P, T // 4], I32, name="scale_rows", tag="grouped0", align_bytes=64)
        fade_col = sb.tile([P, HALVES, FADE_RUN], F32, name="fade_col")
        rate_col = sb.tile([P, RATE_RUN], F32, name="rate_col")
        key = [sb.tile([P, U], F32, name="key%d" % t, tag="key%d" % t) for t in range(TILES)]
        last = TILES - 1
        old_whole = [sb.tile([P, V], F32, name="old%d" % t) for t in range(last)]
        old_last = [sb.tile([P, BANK], F32, name="old_last%d" % h, tag="old_last%d" % h) for h in range(HALVES)]
        ident = sb.tile([P, P], F32, name="ident")

        for j in range(4):
            nc.sync.dma_start(out=scale_rows[j:P:32, :], in_=lat_scales[0, j:16:4, :].bitcast(I32))
        nc.sync.dma_start(lat_list[:], offs)
        nc.sync.dma_start(out=fade_col[:], in_=fade.rearrange("o (h p j) -> p (o h) j", h=HALVES, j=FADE_RUN))
        nc.sync.dma_start(out=rate_col[:], in_=rate.rearrange("o (p j) -> p (o j)", j=RATE_RUN))
        nc.sync.dma_start(out=up_raw[:], in_=up.rearrange("(p j) d -> p j d", j=PACK))
        nc.sync.dma_start(out=words[:].bitcast(I32), in_=lat_words[0].rearrange("p n j -> p (n j)").bitcast(I32))
        nc.sync.dma_start(out=old_whole[0][:], in_=old[rows(0), :])
        nc.sync.dma_start(key_list[:], offs2)
        nc.sync.dma_start(out=key[0][:], in_=keys[rows(0), :])
        nc.sync.dma_start(place_list[:], offs3)
        for t in range(1, TILES):
            nc.sync.dma_start(out=key[t][:], in_=keys[rows(t), :])
        for t in range(1, last):
            nc.sync.dma_start(out=old_whole[t][:], in_=old[rows(t), :])
        for h in range(HALVES):
            nc.sync.dma_start(out=old_last[h][:], in_=old[rows(last), half(h)])

        nc.vector.memset(scales[:].bitcast(I32), 0)
        make_identity(nc, ident[:])
        rate_ps = ps.tile([P, RATE_RUN, P], F32, name="rate_ps")
        for j in range(RATE_RUN):
            nc.tensor.transpose(rate_ps[:, j, :], rate_col[:, j : j + 1].to_broadcast([P, P]), ident[:])
        fade_ps = [ps.tile([P, FADE_RUN, P], F32, name="fade_ps%d" % h) for h in range(HALVES)]
        for h in range(HALVES):
            for j in range(FADE_RUN):
                nc.tensor.transpose(fade_ps[h][:, j, :], fade_col[:, h, j : j + 1].to_broadcast([P, P]), ident[:])

        for q in range(QUADRANTS):
            nc.vector.tensor_copy(scales[32 * q : 32 * q + 4, :].bitcast(I32), scale_rows[32 * q : 32 * q + 4, :])
        lat_s = sb.tile([P, SLOTS], U8, name="lat_s", align_bytes=64)
        nc.vector.tensor_copy(lat_s[:], scales[:].indirect(lat_list[:]))

        grouped = [sb.tile([P, UP_COLS, PACK], BF16, name="grouped%d" % c, tag="grouped%d" % c, align_bytes=64) for c in range(2)]
        up_q = [sb.tile([P, UP_COLS], U32, name="up_q%d" % c, tag="up_q%d" % c, align_bytes=64) for c in range(2)]
        up_s = [sb.tile([P, UP_COLS], U8, name="up_s%d" % c, align_bytes=64) for c in range(2)]
        for c, copy in enumerate((nc.vector.tensor_copy, nc.scalar.copy)):
            copy(
                out=grouped[c][:].rearrange("p (w i) j -> p w j i", i=4),
                in_=up_raw[:, :, c * UP_COLS : (c + 1) * UP_COLS].rearrange("p j (w i) -> p w j i", i=4),
            )
        for c in range(2):
            nc.vector.quantize_mx(out=up_q[c][:].bitcast(FP8X4), scales=up_s[c][:], in_=grouped[c][:].rearrange("p w j -> p (w j)"))

        lat_q = sb.tile([P, SLOTS], U32, name="lat_q", tag="grouped1", align_bytes=64)
        nc.vector.tensor_copy(lat_q[:], words[:].indirect(lat_list[:]))

        z_early = [ps.tile([P, SLOTS], F32, name="z%d" % t) for t in range(EARLY)]
        z_late = ps.tile([P, TILES - EARLY, SLOTS], F32, name="z_late")
        for t in range(TILES):
            cols = rows(t % 2)
            nc.tensor.matmul_mx(
                out=z_early[t][:] if t < EARLY else z_late[:, t - EARLY, :],
                lhsT=up_q[t // 2][:, cols].bitcast(FP8X4),
                lhsT_scale=up_s[t // 2][:, cols],
                rhs=lat_q[:].bitcast(FP8X4),
                rhs_scale=lat_s[:],
                start=True,
                stop=True,
            )

        rf = [sb.tile([P, V], F32, name="rf%d" % t) for t in range(EARLY)]
        rf.extend([sb.tile([P, V], F32, name="rf%d" % (EARLY + c), tag="up_q%d" % c, align_bytes=64) for c in range(2)])
        for t in range(TILES):
            (nc.vector if t < EARLY else nc.gpsimd).memset(rf[t][:], 0.0)

        picked = [sb.tile([P, SLOTS], F32, name="picked%d" % t) for t in range(EARLY)]
        for t in range(EARLY):
            nc.scalar.activation(picked[t][:], key[t][:].indirect(key_list[:]), COPY)
        z_sb = sb.tile([P, TILES - EARLY, SLOTS], F32, name="z_sb", tag="key0")
        nc.scalar.activation(z_sb[:], z_late[:], COPY)

        def remainder(t):
            diff = sb.tile([P, SLOTS], F32, name="diff%d" % t)
            if t < EARLY:
                nc.vector.tensor_tensor(diff[:], picked[t][:], z_early[t][:], ALU.subtract)
            else:
                nc.vector.tensor_tensor(diff[:], key[t][:].indirect(key_list[:]), z_sb[:, t - EARLY, :], ALU.subtract)
            rm = sb.tile([P, SLOTS], F32, name="rm%d" % t)
            nc.vector.tensor_tensor(
                rm[:].rearrange("q (p j) -> q p j", j=RATE_RUN),
                diff[:].rearrange("q (p j) -> q p j", j=RATE_RUN),
                rate_ps[:].rearrange("q j p -> q p j"),
                ALU.mult,
            )
            nc.scalar.activation(rf[t][:].indirect(place_list[:]), rm[:], COPY)

        def fading(t):
            faded = sb.tile([P, V], F32, name="faded%d" % t)
            for h in range(HALVES):
                src = old_last[h][:] if t == last else old_whole[t][:, half(h)]
                nc.vector.tensor_tensor(
                    faded[:, half(h)].rearrange("q (p j) -> q p j", j=FADE_RUN),
                    src.rearrange("q (p j) -> q p j", j=FADE_RUN),
                    fade_ps[h][:].rearrange("q j p -> q p j"),
                    ALU.mult,
                )
            return faded

        faded = [fading(0)]
        for t in range(TILES):
            remainder(t)
        faded.extend([fading(t) for t in range(1, TILES)])

        for t in range(TILES):
            for h in range(HALVES):
                res = sb.tile([P, BANK], F32, name="res%d_%d" % (t, h), tag="old_last%d" % h if t == EARLY else "res%d_%d" % (t, h))
                engine = nc.gpsimd if t < EARLY else nc.vector
                engine.tensor_tensor(res[:], faded[t][:, half(h)], rf[t][:, half(h)], ALU.add)
                nc.sync.dma_start(out=out[rows(t), half(h)], in_=res[:])
